import numpy as np
import ml_dtypes


def mxq(x, axis, fmt="e4m3"):
    dtype, down = {"e4m3": (ml_dtypes.float8_e4m3fn, 7), "e5m2": (ml_dtypes.float8_e5m2, 14)}[fmt]
    v = np.moveaxis(np.asarray(x, np.float32).astype(ml_dtypes.bfloat16).astype(np.float64), axis, -1)
    blocks = v.reshape(v.shape[:-1] + (-1, 32))
    amax = np.abs(blocks).max(-1, keepdims=True)
    byte = np.maximum(np.where(amax > 0, np.frexp(amax)[1] - 1 + 127, 0) - down, 1)
    scale = np.exp2(byte - 127.0)
    codes = (blocks / scale).astype(np.float32).astype(dtype).astype(np.float64)
    return np.moveaxis((codes * scale).reshape(v.shape), -1, axis)


WIDE = False


def mx_kscale(k):
    if not WIDE:
        return np.ones(k)
    levels = np.array([10, -10, 5, -5, 0])
    if k % 512:
        return np.exp2(np.random.permutation(np.resize(levels, k // 32))).repeat(32)
    a = np.empty((k // 512, 16))
    for p in range(k // 512):
        a[p, :8] = np.random.permutation(np.resize(levels, 8))
        for g in range(8):
            far = levels[np.abs(levels - a[p, g]) >= 10]
            a[p, g + 8] = far[np.random.randint(len(far))]
    return np.exp2(a.ravel()).repeat(32)


def f64(x):
    return np.asarray(x).astype(np.float64)


def striped(idx):
    return np.tile(idx.reshape(-1, 16).T, (8, 1)).astype(np.uint16)


def unstriped(offs):
    return offs[:16].T.reshape(-1).astype(np.int64)


def pack_weight(w):
    k, n = w.shape
    w = f64(np.asarray(w, np.float32).astype(ml_dtypes.bfloat16)).reshape(k // 32, 32, n)
    amax = np.abs(w).max(1)
    byte = np.clip(np.where(amax > 0, np.frexp(amax)[1] - 1 + 127 - 7, 1), 1, 254)
    scaled = (w * np.exp2(127.0 - byte)[:, None, :]).reshape(k, n).astype(np.float32)
    words = np.ascontiguousarray(scaled.reshape(k // 512, 128, 4, n).transpose(0, 1, 3, 2)).astype(ml_dtypes.float8_e4m3fn).view(np.uint8)
    return words, np.ascontiguousarray(byte.astype(np.uint8).reshape(k // 512, 16, n))


def unpack_weight(words, scales):
    g, p, n, _ = words.shape
    vals = np.ascontiguousarray(words).view(ml_dtypes.float8_e4m3fn).astype(np.float64) * np.repeat(np.exp2(scales.astype(np.float64) - 127.0), 8, axis=1)[..., None]
    return vals.transpose(0, 1, 3, 2).reshape(g * 512, n)


K, T, S, N, U = 512, 2048, 1024, 128, 2048


def setup_inputs():
    n = np.random.standard_normal
    s = mx_kscale(K)[:, None]
    packed_xT = pack_weight(n((K, T)) * s)
    return {
        "x_words": packed_xT[0],
        "x_scales": packed_xT[1],
        "mem": n((N, U)).astype(np.float32),
        "w1": (n((K, N)) / np.sqrt(K) / s).astype(np.float32),
        "offs": striped(np.random.permutation(T)[:S]),
        "slot": striped(np.random.permutation(U)[:S]),
    }


def reference(x_words, x_scales, mem, w1, offs, slot):
    xq = unpack_weight(x_words, x_scales)[:, unstriped(offs)]
    y = mxq(f64(w1), 0, "e4m3").T @ xq
    out = f64(mem).copy()
    out[:, unstriped(slot)] = f64(mem)[:, unstriped(slot)] + y
    return out

@@ -1,0 +1,67 @@
+from contextlib import ExitStack
+
+import concourse.mybir as mybir
+
+K, T, S, N, U = 512, 2048, 1024, 128, 2048
+FLOPS = 2 * K * N * S
+
+F32 = mybir.dt.float32
+BF16 = mybir.dt.bfloat16
+I32 = mybir.dt.int32
+U32 = mybir.dt.uint32
+U16 = mybir.dt.uint16
+U8 = mybir.dt.uint8
+FP8X4 = mybir.dt.float8_e4m3fn_x4
+
+P = 128
+PACK = 4
+HALF = 512
+LANES = 16
+
+
+def tile_picked_idxput_add_p_kernel(tc, x_words, x_scales, mem, w1, offs, slot, out):
+    nc = tc.nc
+    with ExitStack() as ctx:
+        pool = ctx.enter_context(tc.tile_pool(name="pool", bufs=1))
+        psum = ctx.enter_context(tc.psum_pool(name="psum", bufs=1))
+
+        offs_sb = pool.tile([P, S // LANES], U16, name="offs_sb")
+        slot_sb = pool.tile([P, S // LANES], U16, name="slot_sb")
+        scale_table = pool.tile([P, T], U8, name="scale_table", align_bytes=64)
+        word_table = pool.tile([P, T], I32, name="word_table", align_bytes=64)
+        w_raw = pool.tile([P, PACK, N], F32, name="w_raw", tag="w_then_store", align_bytes=64)
+
+        nc.vector.memset(scale_table[:].bitcast(I32), 0)
+        nc.sync.dma_start(offs_sb[:], offs)
+        nc.sync.dma_start(w_raw[:], w1.rearrange("(p j) n -> p j n", j=PACK))
+        for q in range(4):
+            nc.scalar.dma_start(scale_table[32 * q : 32 * q + 4, :].bitcast(I32), x_scales[0, 4 * q : 4 * q + 4, :].bitcast(I32))
+        nc.sync.dma_start(word_table[:], x_words[0].rearrange("p n t -> p (n t)").bitcast(I32))
+        nc.sync.dma_start(slot_sb[:], slot)
+
+        w_grouped = pool.tile([P, N, PACK], BF16, name="w_grouped", align_bytes=64)
+        nc.scalar.copy(w_grouped[:], w_raw[:].rearrange("p j n -> p n j"))
+        store = pool.tile([P, U], F32, name="store", tag="w_then_store", align_bytes=64)
+        nc.sync.dma_start(store[:], mem)
+
+        x_scale = pool.tile([P, S], U8, name="x_scale", align_bytes=64)
+        nc.vector.tensor_copy(x_scale[:], scale_table[:].indirect(offs_sb[:]))
+
+        w_code = pool.tile([P, N], U32, name="w_code", align_bytes=64)
+        w_scale = pool.tile([P, N], U8, name="w_scale", align_bytes=64)
+        nc.vector.quantize_mx(out=w_code[:].bitcast(FP8X4), scales=w_scale[:], in_=w_grouped[:].rearrange("p n j -> p (n j)"))
+
+        y = pool.tile([P, S], F32, name="y", align_bytes=64)
+        for h in range(S // HALF):
+            cols = slice(h * HALF, (h + 1) * HALF)
+            x_code = pool.tile([P, HALF], U32, name=f"x_code{h}", align_bytes=64)
+            nc.vector.tensor_copy(x_code[:], word_table[:].bitcast(U32).indirect(offs_sb[:, h * HALF // LANES : (h + 1) * HALF // LANES]))
+            acc = psum.tile([P, HALF], F32, name=f"acc{h}")
+            nc.tensor.matmul_mx(out=acc[:], lhsT=w_code[:].bitcast(FP8X4), lhsT_scale=w_scale[:],
+                                rhs=x_code[:].bitcast(FP8X4), rhs_scale=x_scale[:, cols], start=True, stop=True)
+            nc.scalar.copy(y[:, cols], acc[:])
+
+        old = pool.tile([P, S], F32, name="old", align_bytes=64)
+        nc.vector.tensor_copy(old[:], store[:].indirect(slot_sb[:]))
+        nc.vector.tensor_tensor(store[:].indirect(slot_sb[:]), old[:], y[:], mybir.AluOpType.add)
+        nc.sync.dma_start(out, store[:])

@@ -29,20 +29,21 @@ def tile_picked_idxput_add_p_kernel(tc, x_words, x_scales, mem, w1, offs, slot, 
         slot_sb = pool.tile([P, S // LANES], U16, name="slot_sb")
         scale_table = pool.tile([P, T], U8, name="scale_table", align_bytes=64)
         word_table = pool.tile([P, T], I32, name="word_table", align_bytes=64)
-        w_raw = pool.tile([P, PACK, N], F32, name="w_raw", tag="w_then_store", align_bytes=64)
+        store = pool.tile([P, U], F32, name="store", align_bytes=64)
+        w_raw = pool.tile([P, PACK, N], F32, name="w_raw", align_bytes=64)
 
         nc.vector.memset(scale_table[:].bitcast(I32), 0)
         nc.sync.dma_start(offs_sb[:], offs)
         nc.sync.dma_start(w_raw[:], w1.rearrange("(p j) n -> p j n", j=PACK))
         for q in range(4):
-            nc.scalar.dma_start(scale_table[32 * q : 32 * q + 4, :].bitcast(I32), x_scales[0, 4 * q : 4 * q + 4, :].bitcast(I32))
+            queue = nc.sync if q < 2 else nc.scalar
+            queue.dma_start(scale_table[32 * q : 32 * q + 4, :].bitcast(I32), x_scales[0, 4 * q : 4 * q + 4, :].bitcast(I32))
         nc.sync.dma_start(word_table[:], x_words[0].rearrange("p n t -> p (n t)").bitcast(I32))
         nc.sync.dma_start(slot_sb[:], slot)
+        nc.sync.dma_start(store[:], mem)
 
         w_grouped = pool.tile([P, N, PACK], BF16, name="w_grouped", align_bytes=64)
         nc.scalar.copy(w_grouped[:], w_raw[:].rearrange("p j n -> p n j"))
-        store = pool.tile([P, U], F32, name="store", tag="w_then_store", align_bytes=64)
-        nc.sync.dma_start(store[:], mem)
 
         x_scale = pool.tile([P, S], U8, name="x_scale", align_bytes=64)
         nc.vector.tensor_copy(x_scale[:], scale_table[:].indirect(offs_sb[:]))

@@ -32,12 +32,12 @@ def tile_picked_idxput_add_p_kernel(tc, x_words, x_scales, mem, w1, offs, slot, 
         store = pool.tile([P, U], F32, name="store", align_bytes=64)
         w_raw = pool.tile([P, PACK, N], F32, name="w_raw", align_bytes=64)
 
+        x_scale = pool.tile([P, S], U8, name="x_scale", align_bytes=64)
         nc.vector.memset(scale_table[:].bitcast(I32), 0)
+        nc.vector.memset(x_scale[:].bitcast(I32), 0)
         nc.sync.dma_start(offs_sb[:], offs)
         nc.sync.dma_start(w_raw[:], w1.rearrange("(p j) n -> p j n", j=PACK))
-        for q in range(4):
-            queue = nc.sync if q < 2 else nc.scalar
-            queue.dma_start(scale_table[32 * q : 32 * q + 4, :].bitcast(I32), x_scales[0, 4 * q : 4 * q + 4, :].bitcast(I32))
+        nc.sync.dma_start(scale_table[0:P:8, :].bitcast(I32), x_scales[0].bitcast(I32))
         nc.sync.dma_start(word_table[:], x_words[0].rearrange("p n t -> p (n t)").bitcast(I32))
         nc.sync.dma_start(slot_sb[:], slot)
         nc.sync.dma_start(store[:], mem)
@@ -45,21 +45,24 @@ def tile_picked_idxput_add_p_kernel(tc, x_words, x_scales, mem, w1, offs, slot, 
         w_grouped = pool.tile([P, N, PACK], BF16, name="w_grouped", align_bytes=64)
         nc.scalar.copy(w_grouped[:], w_raw[:].rearrange("p j n -> p n j"))
 
-        x_scale = pool.tile([P, S], U8, name="x_scale", align_bytes=64)
-        nc.vector.tensor_copy(x_scale[:], scale_table[:].indirect(offs_sb[:]))
+        picked_scale = pool.tile([P, S], U8, name="picked_scale", align_bytes=64)
+        nc.vector.tensor_copy(picked_scale[:], scale_table[:].indirect(offs_sb[:]))
+        for q in range(4):
+            nc.scalar.dma_start(x_scale[32 * q : 32 * q + 4, :].bitcast(I32), picked_scale[32 * q : 32 * q + 32 : 8, :].bitcast(I32))
 
         w_code = pool.tile([P, N], U32, name="w_code", align_bytes=64)
         w_scale = pool.tile([P, N], U8, name="w_scale", align_bytes=64)
         nc.vector.quantize_mx(out=w_code[:].bitcast(FP8X4), scales=w_scale[:], in_=w_grouped[:].rearrange("p n j -> p (n j)"))
 
+        x_code = pool.tile([P, S], U32, name="x_code", align_bytes=64)
+        nc.vector.tensor_copy(x_code[:], word_table[:].bitcast(U32).indirect(offs_sb[:]))
+
         y = pool.tile([P, S], F32, name="y", align_bytes=64)
         for h in range(S // HALF):
             cols = slice(h * HALF, (h + 1) * HALF)
-            x_code = pool.tile([P, HALF], U32, name=f"x_code{h}", align_bytes=64)
-            nc.vector.tensor_copy(x_code[:], word_table[:].bitcast(U32).indirect(offs_sb[:, h * HALF // LANES : (h + 1) * HALF // LANES]))
             acc = psum.tile([P, HALF], F32, name=f"acc{h}")
             nc.tensor.matmul_mx(out=acc[:], lhsT=w_code[:].bitcast(FP8X4), lhsT_scale=w_scale[:],
-                                rhs=x_code[:].bitcast(FP8X4), rhs_scale=x_scale[:, cols], start=True, stop=True)
+                                rhs=x_code[:, cols].bitcast(FP8X4), rhs_scale=x_scale[:, cols], start=True, stop=True)
             nc.scalar.copy(y[:, cols], acc[:])
 
         old = pool.tile([P, S], F32, name="old", align_bytes=64)

@@ -33,11 +33,11 @@ def tile_picked_idxput_add_p_kernel(tc, x_words, x_scales, mem, w1, offs, slot, 
         w_raw = pool.tile([P, PACK, N], F32, name="w_raw", align_bytes=64)
 
         x_scale = pool.tile([P, S], U8, name="x_scale", align_bytes=64)
-        nc.vector.memset(scale_table[:].bitcast(I32), 0)
+        nc.vector.memset(scale_table[0:112, :].bitcast(I32), 0)
         nc.vector.memset(x_scale[:].bitcast(I32), 0)
         nc.sync.dma_start(offs_sb[:], offs)
+        nc.sync.dma_start(scale_table[112:P, :].bitcast(I32), x_scales[0].bitcast(I32))
         nc.sync.dma_start(w_raw[:], w1.rearrange("(p j) n -> p j n", j=PACK))
-        nc.sync.dma_start(scale_table[0:P:8, :].bitcast(I32), x_scales[0].bitcast(I32))
         nc.sync.dma_start(word_table[:], x_words[0].rearrange("p n t -> p (n t)").bitcast(I32))
         nc.sync.dma_start(slot_sb[:], slot)
         nc.sync.dma_start(store[:], mem)
@@ -48,7 +48,7 @@ def tile_picked_idxput_add_p_kernel(tc, x_words, x_scales, mem, w1, offs, slot, 
         picked_scale = pool.tile([P, S], U8, name="picked_scale", align_bytes=64)
         nc.vector.tensor_copy(picked_scale[:], scale_table[:].indirect(offs_sb[:]))
         for q in range(4):
-            nc.scalar.dma_start(x_scale[32 * q : 32 * q + 4, :].bitcast(I32), picked_scale[32 * q : 32 * q + 32 : 8, :].bitcast(I32))
+            nc.scalar.dma_start(x_scale[32 * q : 32 * q + 4, :].bitcast(I32), picked_scale[112 + 4 * q : 116 + 4 * q, :].bitcast(I32))
 
         w_code = pool.tile([P, N], U32, name="w_code", align_bytes=64)
         w_scale = pool.tile([P, N], U8, name="w_scale", align_bytes=64)
@@ -68,4 +68,5 @@ def tile_picked_idxput_add_p_kernel(tc, x_words, x_scales, mem, w1, offs, slot, 
         old = pool.tile([P, S], F32, name="old", align_bytes=64)
         nc.vector.tensor_copy(old[:], store[:].indirect(slot_sb[:]))
         nc.vector.tensor_tensor(store[:].indirect(slot_sb[:]), old[:], y[:], mybir.AluOpType.add)
-        nc.sync.dma_start(out, store[:])
+        nc.sync.dma_start(out[:, : U // 2], store[:, : U // 2])
+        nc.scalar.dma_start(out[:, U // 2 :], store[:, U // 2 :])

@@ -15,7 +15,7 @@ FP8X4 = mybir.dt.float8_e4m3fn_x4
 
 P = 128
 PACK = 4
-HALF = 512
+HALF = 256
 LANES = 16
 
 
@@ -27,12 +27,12 @@ def tile_picked_idxput_add_p_kernel(tc, x_words, x_scales, mem, w1, offs, slot, 
 
         offs_sb = pool.tile([P, S // LANES], U16, name="offs_sb")
         slot_sb = pool.tile([P, S // LANES], U16, name="slot_sb")
-        scale_table = pool.tile([P, T], U8, name="scale_table", align_bytes=64)
-        word_table = pool.tile([P, T], I32, name="word_table", align_bytes=64)
-        store = pool.tile([P, U], F32, name="store", align_bytes=64)
-        w_raw = pool.tile([P, PACK, N], F32, name="w_raw", align_bytes=64)
+        scale_table = pool.tile([P, T], U8, name="scale_table", align_bytes=256)
+        word_table = pool.tile([P, T], I32, name="word_table", align_bytes=256)
+        store = pool.tile([P, U], F32, name="store", align_bytes=256)
+        w_raw = pool.tile([P, PACK, N], F32, name="w_raw", align_bytes=256)
 
-        x_scale = pool.tile([P, S], U8, name="x_scale", align_bytes=64)
+        x_scale = pool.tile([P, S], U8, name="x_scale", align_bytes=256)
         nc.vector.memset(scale_table[0:112, :].bitcast(I32), 0)
         nc.vector.memset(x_scale[:].bitcast(I32), 0)
         nc.sync.dma_start(offs_sb[:], offs)
@@ -42,22 +42,22 @@ def tile_picked_idxput_add_p_kernel(tc, x_words, x_scales, mem, w1, offs, slot, 
         nc.sync.dma_start(slot_sb[:], slot)
         nc.sync.dma_start(store[:], mem)
 
-        w_grouped = pool.tile([P, N, PACK], BF16, name="w_grouped", align_bytes=64)
+        w_grouped = pool.tile([P, N, PACK], BF16, name="w_grouped", align_bytes=256)
         nc.scalar.copy(w_grouped[:], w_raw[:].rearrange("p j n -> p n j"))
 
-        picked_scale = pool.tile([P, S], U8, name="picked_scale", align_bytes=64)
+        picked_scale = pool.tile([P, S], U8, name="picked_scale", align_bytes=256)
         nc.vector.tensor_copy(picked_scale[:], scale_table[:].indirect(offs_sb[:]))
         for q in range(4):
-            nc.scalar.dma_start(x_scale[32 * q : 32 * q + 4, :].bitcast(I32), picked_scale[112 + 4 * q : 116 + 4 * q, :].bitcast(I32))
+            nc.sync.dma_start(x_scale[32 * q : 32 * q + 4, :].bitcast(I32), picked_scale[112 + 4 * q : 116 + 4 * q, :].bitcast(I32))
 
-        w_code = pool.tile([P, N], U32, name="w_code", align_bytes=64)
-        w_scale = pool.tile([P, N], U8, name="w_scale", align_bytes=64)
+        w_code = pool.tile([P, N], U32, name="w_code", align_bytes=256)
+        w_scale = pool.tile([P, N], U8, name="w_scale", align_bytes=256)
         nc.vector.quantize_mx(out=w_code[:].bitcast(FP8X4), scales=w_scale[:], in_=w_grouped[:].rearrange("p n j -> p (n j)"))
 
-        x_code = pool.tile([P, S], U32, name="x_code", align_bytes=64)
+        x_code = pool.tile([P, S], U32, name="x_code", align_bytes=256)
         nc.vector.tensor_copy(x_code[:], word_table[:].bitcast(U32).indirect(offs_sb[:]))
 
-        y = pool.tile([P, S], F32, name="y", align_bytes=64)
+        y = pool.tile([P, S], F32, name="y", align_bytes=256)
         for h in range(S // HALF):
             cols = slice(h * HALF, (h + 1) * HALF)
             acc = psum.tile([P, HALF], F32, name=f"acc{h}")
@@ -65,8 +65,7 @@ def tile_picked_idxput_add_p_kernel(tc, x_words, x_scales, mem, w1, offs, slot, 
                                 rhs=x_code[:, cols].bitcast(FP8X4), rhs_scale=x_scale[:, cols], start=True, stop=True)
             nc.scalar.copy(y[:, cols], acc[:])
 
-        old = pool.tile([P, S], F32, name="old", align_bytes=64)
+        old = pool.tile([P, S], F32, name="old", align_bytes=256)
         nc.vector.tensor_copy(old[:], store[:].indirect(slot_sb[:]))
         nc.vector.tensor_tensor(store[:].indirect(slot_sb[:]), old[:], y[:], mybir.AluOpType.add)
-        nc.sync.dma_start(out[:, : U // 2], store[:, : U // 2])
-        nc.scalar.dma_start(out[:, U // 2 :], store[:, U // 2 :])
+        nc.sync.dma_start(out, store[:])

@@ -36,9 +36,9 @@ def tile_picked_idxput_add_p_kernel(tc, x_words, x_scales, mem, w1, offs, slot, 
         nc.vector.memset(scale_table[0:112, :].bitcast(I32), 0)
         nc.vector.memset(x_scale[:].bitcast(I32), 0)
         nc.sync.dma_start(offs_sb[:], offs)
-        nc.sync.dma_start(scale_table[112:P, :].bitcast(I32), x_scales[0].bitcast(I32))
-        nc.sync.dma_start(w_raw[:], w1.rearrange("(p j) n -> p j n", j=PACK))
+        nc.scalar.dma_start(scale_table[112:P, :].bitcast(I32), x_scales[0].bitcast(I32))
         nc.sync.dma_start(word_table[:], x_words[0].rearrange("p n t -> p (n t)").bitcast(I32))
+        nc.sync.dma_start(w_raw[:], w1.rearrange("(p j) n -> p j n", j=PACK))
         nc.sync.dma_start(slot_sb[:], slot)
         nc.sync.dma_start(store[:], mem)
 

@@ -47,8 +47,9 @@ def tile_picked_idxput_add_p_kernel(tc, x_words, x_scales, mem, w1, offs, slot, 
 
         picked_scale = pool.tile([P, S], U8, name="picked_scale", align_bytes=256)
         nc.vector.tensor_copy(picked_scale[:], scale_table[:].indirect(offs_sb[:]))
-        for q in range(4):
-            nc.sync.dma_start(x_scale[32 * q : 32 * q + 4, :].bitcast(I32), picked_scale[112 + 4 * q : 116 + 4 * q, :].bitcast(I32))
+        moves = [(0, slice(0, S))] + [(q, cols) for cols in (slice(0, S // 2), slice(S // 2, S)) for q in range(1, 4)]
+        for q, cols in moves:
+            nc.sync.dma_start(x_scale[32 * q : 32 * q + 4, cols].bitcast(I32), picked_scale[112 + 4 * q : 116 + 4 * q, cols].bitcast(I32))
 
         w_code = pool.tile([P, N], U32, name="w_code", align_bytes=256)
         w_scale = pool.tile([P, N], U8, name="w_scale", align_bytes=256)
@@ -68,4 +69,5 @@ def tile_picked_idxput_add_p_kernel(tc, x_words, x_scales, mem, w1, offs, slot, 
         old = pool.tile([P, S], F32, name="old", align_bytes=256)
         nc.vector.tensor_copy(old[:], store[:].indirect(slot_sb[:]))
         nc.vector.tensor_tensor(store[:].indirect(slot_sb[:]), old[:], y[:], mybir.AluOpType.add)
-        nc.sync.dma_start(out, store[:])
+        for cols in (slice(0, U // 2), slice(U // 2, U)):
+            nc.sync.dma_start(out[:, cols], store[:, cols])

@@ -15,7 +15,8 @@ FP8X4 = mybir.dt.float8_e4m3fn_x4
 
 P = 128
 PACK = 4
-HALF = 256
+TAIL = 64
+EDGES = (0, 256, 512, 768, 896, 960, 1024)
 LANES = 16
 
 
@@ -59,15 +60,18 @@ def tile_picked_idxput_add_p_kernel(tc, x_words, x_scales, mem, w1, offs, slot, 
         nc.vector.tensor_copy(x_code[:], word_table[:].bitcast(U32).indirect(offs_sb[:]))
 
         y = pool.tile([P, S], F32, name="y", align_bytes=256)
-        for h in range(S // HALF):
-            cols = slice(h * HALF, (h + 1) * HALF)
-            acc = psum.tile([P, HALF], F32, name=f"acc{h}")
+        y_tail = pool.tile([P, TAIL], F32, name="y_tail", align_bytes=256)
+        nc.vector.memset(y[:, S - TAIL :], 0.0)
+        for lo, hi in zip(EDGES, EDGES[1:]):
+            cols = slice(lo, hi)
+            acc = psum.tile([P, hi - lo], F32, name=f"acc{lo}")
             nc.tensor.matmul_mx(out=acc[:], lhsT=w_code[:].bitcast(FP8X4), lhsT_scale=w_scale[:],
                                 rhs=x_code[:, cols].bitcast(FP8X4), rhs_scale=x_scale[:, cols], start=True, stop=True)
-            nc.scalar.copy(y[:, cols], acc[:])
+            nc.scalar.copy(y[:, cols] if hi < S else y_tail[:], acc[:])
 
         old = pool.tile([P, S], F32, name="old", align_bytes=256)
-        nc.vector.tensor_copy(old[:], store[:].indirect(slot_sb[:]))
+        nc.vector.tensor_copy(old[:, : S - TAIL], store[:].indirect(slot_sb[:, : (S - TAIL) // LANES]))
+        nc.vector.tensor_tensor(old[:, S - TAIL :], store[:].indirect(slot_sb[:, (S - TAIL) // LANES :]), y_tail[:], mybir.AluOpType.add)
         nc.vector.tensor_tensor(store[:].indirect(slot_sb[:]), old[:], y[:], mybir.AluOpType.add)
         for cols in (slice(0, U // 2), slice(U // 2, U)):
             nc.sync.dma_start(out[:, cols], store[:, cols])

@@ -15,9 +15,14 @@ FP8X4 = mybir.dt.float8_e4m3fn_x4
 
 P = 128
 PACK = 4
-TAIL = 64
-EDGES = (0, 256, 512, 768, 896, 960, 1024)
 LANES = 16
+QUADRANTS, QUADRANT = 4, 32
+ROWS = 4
+TABLE_ROW = P - K // 32
+ALIGN = 256
+PIECE = S // 8
+TAIL = 64
+HEAD = S - TAIL
 
 
 def tile_picked_idxput_add_p_kernel(tc, x_words, x_scales, mem, w1, offs, slot, out):
@@ -28,50 +33,57 @@ def tile_picked_idxput_add_p_kernel(tc, x_words, x_scales, mem, w1, offs, slot, 
 
         offs_sb = pool.tile([P, S // LANES], U16, name="offs_sb")
         slot_sb = pool.tile([P, S // LANES], U16, name="slot_sb")
-        scale_table = pool.tile([P, T], U8, name="scale_table", align_bytes=256)
-        word_table = pool.tile([P, T], I32, name="word_table", align_bytes=256)
-        store = pool.tile([P, U], F32, name="store", align_bytes=256)
-        w_raw = pool.tile([P, PACK, N], F32, name="w_raw", align_bytes=256)
+        scale_table = pool.tile([P, T], U8, name="scale_table", align_bytes=ALIGN)
+        word_table = pool.tile([P, T], I32, name="word_table", align_bytes=ALIGN)
+        store = pool.tile([P, U], F32, name="store", align_bytes=ALIGN)
+        w_raw = pool.tile([P, PACK, N], F32, name="w_raw", align_bytes=ALIGN)
+        x_scale = pool.tile([P, S], U8, name="x_scale", align_bytes=ALIGN)
 
-        x_scale = pool.tile([P, S], U8, name="x_scale", align_bytes=256)
-        nc.vector.memset(scale_table[0:112, :].bitcast(I32), 0)
+        nc.vector.memset(scale_table[0:TABLE_ROW, :].bitcast(I32), 0)
         nc.vector.memset(x_scale[:].bitcast(I32), 0)
+
         nc.sync.dma_start(offs_sb[:], offs)
-        nc.scalar.dma_start(scale_table[112:P, :].bitcast(I32), x_scales[0].bitcast(I32))
+        nc.scalar.dma_start(scale_table[TABLE_ROW:P, :].bitcast(I32), x_scales[0].bitcast(I32))
         nc.sync.dma_start(word_table[:], x_words[0].rearrange("p n t -> p (n t)").bitcast(I32))
         nc.sync.dma_start(w_raw[:], w1.rearrange("(p j) n -> p j n", j=PACK))
         nc.sync.dma_start(slot_sb[:], slot)
         nc.sync.dma_start(store[:], mem)
 
-        w_grouped = pool.tile([P, N, PACK], BF16, name="w_grouped", align_bytes=256)
+        w_grouped = pool.tile([P, N, PACK], BF16, name="w_grouped", align_bytes=ALIGN)
         nc.scalar.copy(w_grouped[:], w_raw[:].rearrange("p j n -> p n j"))
 
-        picked_scale = pool.tile([P, S], U8, name="picked_scale", align_bytes=256)
+        picked_scale = pool.tile([P, S], U8, name="picked_scale", align_bytes=ALIGN)
         nc.vector.tensor_copy(picked_scale[:], scale_table[:].indirect(offs_sb[:]))
-        moves = [(0, slice(0, S))] + [(q, cols) for cols in (slice(0, S // 2), slice(S // 2, S)) for q in range(1, 4)]
+        moves = [(0, slice(0, S))] + [(q, cols) for cols in (slice(0, S // 2), slice(S // 2, S)) for q in range(1, QUADRANTS)]
         for q, cols in moves:
-            nc.sync.dma_start(x_scale[32 * q : 32 * q + 4, cols].bitcast(I32), picked_scale[112 + 4 * q : 116 + 4 * q, cols].bitcast(I32))
+            src_row, dst_row = TABLE_ROW + ROWS * q, QUADRANT * q
+            nc.sync.dma_start(x_scale[dst_row : dst_row + ROWS, cols].bitcast(I32),
+                              picked_scale[src_row : src_row + ROWS, cols].bitcast(I32))
 
-        w_code = pool.tile([P, N], U32, name="w_code", align_bytes=256)
-        w_scale = pool.tile([P, N], U8, name="w_scale", align_bytes=256)
+        w_code = pool.tile([P, N], U32, name="w_code", align_bytes=ALIGN)
+        w_scale = pool.tile([P, N], U8, name="w_scale", align_bytes=ALIGN)
         nc.vector.quantize_mx(out=w_code[:].bitcast(FP8X4), scales=w_scale[:], in_=w_grouped[:].rearrange("p n j -> p (n j)"))
 
-        x_code = pool.tile([P, S], U32, name="x_code", align_bytes=256)
+        x_code = pool.tile([P, S], U32, name="x_code", align_bytes=ALIGN)
         nc.vector.tensor_copy(x_code[:], word_table[:].bitcast(U32).indirect(offs_sb[:]))
 
-        y = pool.tile([P, S], F32, name="y", align_bytes=256)
-        y_tail = pool.tile([P, TAIL], F32, name="y_tail", align_bytes=256)
-        nc.vector.memset(y[:, S - TAIL :], 0.0)
-        for lo, hi in zip(EDGES, EDGES[1:]):
-            cols = slice(lo, hi)
-            acc = psum.tile([P, hi - lo], F32, name=f"acc{lo}")
+        y = pool.tile([P, S], F32, name="y", align_bytes=ALIGN)
+        y_tail = pool.tile([P, TAIL], F32, name="y_tail", align_bytes=ALIGN)
+        nc.vector.memset(y[:, HEAD:], 0.0)
+        for lo in range(0, S, PIECE):
+            hi = lo + PIECE
+            acc = psum.tile([P, PIECE], F32, name=f"acc{lo}")
             nc.tensor.matmul_mx(out=acc[:], lhsT=w_code[:].bitcast(FP8X4), lhsT_scale=w_scale[:],
-                                rhs=x_code[:, cols].bitcast(FP8X4), rhs_scale=x_scale[:, cols], start=True, stop=True)
-            nc.scalar.copy(y[:, cols] if hi < S else y_tail[:], acc[:])
+                                rhs=x_code[:, lo:hi].bitcast(FP8X4), rhs_scale=x_scale[:, lo:hi], start=True, stop=True)
+            if hi < S:
+                nc.scalar.copy(y[:, lo:hi], acc[:])
+            else:
+                nc.scalar.copy(y[:, lo:HEAD], acc[:, : PIECE - TAIL])
+                nc.scalar.copy(y_tail[:], acc[:, PIECE - TAIL :])
 
-        old = pool.tile([P, S], F32, name="old", align_bytes=256)
-        nc.vector.tensor_copy(old[:, : S - TAIL], store[:].indirect(slot_sb[:, : (S - TAIL) // LANES]))
-        nc.vector.tensor_tensor(old[:, S - TAIL :], store[:].indirect(slot_sb[:, (S - TAIL) // LANES :]), y_tail[:], mybir.AluOpType.add)
+        old = pool.tile([P, S], F32, name="old", align_bytes=ALIGN)
+        nc.vector.tensor_copy(old[:, :HEAD], store[:].indirect(slot_sb[:, : HEAD // LANES]))
+        nc.vector.tensor_tensor(old[:, HEAD:], store[:].indirect(slot_sb[:, HEAD // LANES :]), y_tail[:], mybir.AluOpType.add)
         nc.vector.tensor_tensor(store[:].indirect(slot_sb[:]), old[:], y[:], mybir.AluOpType.add)
         for cols in (slice(0, U // 2), slice(U // 2, U)):
             nc.sync.dma_start(out[:, cols], store[:, cols])

@@ -20,9 +20,9 @@ QUADRANTS, QUADRANT = 4, 32
 ROWS = 4
 TABLE_ROW = P - K // 32
 ALIGN = 256
-PIECE = S // 8
-TAIL = 64
-HEAD = S - TAIL
+CUT = 512
+FIRST = 256
+PIECES = [128,128,256,256,256]
 
 
 def tile_picked_idxput_add_p_kernel(tc, x_words, x_scales, mem, w1, offs, slot, out):
@@ -36,7 +36,7 @@ def tile_picked_idxput_add_p_kernel(tc, x_words, x_scales, mem, w1, offs, slot, 
         scale_table = pool.tile([P, T], U8, name="scale_table", align_bytes=ALIGN)
         word_table = pool.tile([P, T], I32, name="word_table", align_bytes=ALIGN)
         store = pool.tile([P, U], F32, name="store", align_bytes=ALIGN)
-        w_raw = pool.tile([P, PACK, N], F32, name="w_raw", align_bytes=ALIGN)
+        w_raw = pool.tile([P, PACK, N], F32, name="w_raw", tag="staging", align_bytes=ALIGN)
         x_scale = pool.tile([P, S], U8, name="x_scale", align_bytes=ALIGN)
 
         nc.vector.memset(scale_table[0:TABLE_ROW, :].bitcast(I32), 0)
@@ -44,13 +44,13 @@ def tile_picked_idxput_add_p_kernel(tc, x_words, x_scales, mem, w1, offs, slot, 
 
         nc.sync.dma_start(offs_sb[:], offs)
         nc.scalar.dma_start(scale_table[TABLE_ROW:P, :].bitcast(I32), x_scales[0].bitcast(I32))
-        nc.sync.dma_start(word_table[:], x_words[0].rearrange("p n t -> p (n t)").bitcast(I32))
-        nc.sync.dma_start(w_raw[:], w1.rearrange("(p j) n -> p j n", j=PACK))
         nc.sync.dma_start(slot_sb[:], slot)
         nc.sync.dma_start(store[:], mem)
+        nc.sync.dma_start(word_table[:], x_words[0].rearrange("p n t -> p (n t)").bitcast(I32))
+        nc.sync.dma_start(w_raw[:], w1.rearrange("(p j) n -> p j n", j=PACK))
 
         w_grouped = pool.tile([P, N, PACK], BF16, name="w_grouped", align_bytes=ALIGN)
-        nc.scalar.copy(w_grouped[:], w_raw[:].rearrange("p j n -> p n j"))
+        nc.scalar.copy(w_grouped[:].rearrange("p (c i) j -> p c j i", i=4), w_raw[:].rearrange("p j (c i) -> p c j i", i=4))
 
         picked_scale = pool.tile([P, S], U8, name="picked_scale", align_bytes=ALIGN)
         nc.vector.tensor_copy(picked_scale[:], scale_table[:].indirect(offs_sb[:]))
@@ -60,30 +60,30 @@ def tile_picked_idxput_add_p_kernel(tc, x_words, x_scales, mem, w1, offs, slot, 
             nc.sync.dma_start(x_scale[dst_row : dst_row + ROWS, cols].bitcast(I32),
                               picked_scale[src_row : src_row + ROWS, cols].bitcast(I32))
 
+        old = pool.tile([P, S], F32, name="old", align_bytes=ALIGN)
+        nc.vector.tensor_copy(old[:], store[:].indirect(slot_sb[:]))
+
+        early_code = pool.tile([P, CUT], U32, name="early_code", align_bytes=ALIGN)
+        nc.vector.tensor_copy(early_code[:], word_table[:].bitcast(U32).indirect(offs_sb[:, : CUT // LANES]))
         w_code = pool.tile([P, N], U32, name="w_code", align_bytes=ALIGN)
         w_scale = pool.tile([P, N], U8, name="w_scale", align_bytes=ALIGN)
         nc.vector.quantize_mx(out=w_code[:].bitcast(FP8X4), scales=w_scale[:], in_=w_grouped[:].rearrange("p n j -> p (n j)"))
-
-        x_code = pool.tile([P, S], U32, name="x_code", align_bytes=ALIGN)
-        nc.vector.tensor_copy(x_code[:], word_table[:].bitcast(U32).indirect(offs_sb[:]))
+        late_code = pool.tile([P, S - CUT], U32, name="late_code", tag="staging", align_bytes=ALIGN)
+        nc.vector.tensor_copy(late_code[:], word_table[:].bitcast(U32).indirect(offs_sb[:, CUT // LANES :]))
 
         y = pool.tile([P, S], F32, name="y", align_bytes=ALIGN)
-        y_tail = pool.tile([P, TAIL], F32, name="y_tail", align_bytes=ALIGN)
-        nc.vector.memset(y[:, HEAD:], 0.0)
-        for lo in range(0, S, PIECE):
-            hi = lo + PIECE
-            acc = psum.tile([P, PIECE], F32, name=f"acc{lo}")
+        lo = 0
+        for width in PIECES:
+            hi = lo + width
+            code = early_code[:, lo:hi] if hi <= CUT else late_code[:, lo - CUT : hi - CUT]
+            acc = psum.tile([P, width], F32, name=f"acc{lo}")
             nc.tensor.matmul_mx(out=acc[:], lhsT=w_code[:].bitcast(FP8X4), lhsT_scale=w_scale[:],
-                                rhs=x_code[:, lo:hi].bitcast(FP8X4), rhs_scale=x_scale[:, lo:hi], start=True, stop=True)
-            if hi < S:
-                nc.scalar.copy(y[:, lo:hi], acc[:])
-            else:
-                nc.scalar.copy(y[:, lo:HEAD], acc[:, : PIECE - TAIL])
-                nc.scalar.copy(y_tail[:], acc[:, PIECE - TAIL :])
+                                rhs=code.bitcast(FP8X4), rhs_scale=x_scale[:, lo:hi], start=True, stop=True)
+            nc.scalar.copy(y[:, lo:hi], acc[:])
+            lo = hi
 
-        old = pool.tile([P, S], F32, name="old", align_bytes=ALIGN)
-        nc.vector.tensor_copy(old[:, :HEAD], store[:].indirect(slot_sb[:, : HEAD // LANES]))
-        nc.vector.tensor_tensor(old[:, HEAD:], store[:].indirect(slot_sb[:, HEAD // LANES :]), y_tail[:], mybir.AluOpType.add)
-        nc.vector.tensor_tensor(store[:].indirect(slot_sb[:]), old[:], y[:], mybir.AluOpType.add)
+        for lo, hi in ((0, FIRST), (FIRST, S)):
+            nc.vector.tensor_tensor(store[:].indirect(slot_sb[:, lo // LANES : hi // LANES]), old[:, lo:hi], y[:, lo:hi],
+                                    mybir.AluOpType.add)
         for cols in (slice(0, U // 2), slice(U // 2, U)):
             nc.sync.dma_start(out[:, cols], store[:, cols])

@@ -54,7 +54,7 @@ def tile_picked_idxput_add_p_kernel(tc, x_words, x_scales, mem, w1, offs, slot, 
 
         picked_scale = pool.tile([P, S], U8, name="picked_scale", align_bytes=ALIGN)
         nc.vector.tensor_copy(picked_scale[:], scale_table[:].indirect(offs_sb[:]))
-        moves = [(0, slice(0, S))] + [(q, cols) for cols in (slice(0, S // 2), slice(S // 2, S)) for q in range(1, QUADRANTS)]
+        moves = [(q, cols) for cols in (slice(0, CUT), slice(CUT, S)) for q in range(QUADRANTS)]
         for q, cols in moves:
             src_row, dst_row = TABLE_ROW + ROWS * q, QUADRANT * q
             nc.sync.dma_start(x_scale[dst_row : dst_row + ROWS, cols].bitcast(I32),
@@ -85,5 +85,4 @@ def tile_picked_idxput_add_p_kernel(tc, x_words, x_scales, mem, w1, offs, slot, 
         for lo, hi in ((0, FIRST), (FIRST, S)):
             nc.vector.tensor_tensor(store[:].indirect(slot_sb[:, lo // LANES : hi // LANES]), old[:, lo:hi], y[:, lo:hi],
                                     mybir.AluOpType.add)
-        for cols in (slice(0, U // 2), slice(U // 2, U)):
-            nc.sync.dma_start(out[:, cols], store[:, cols])
+        nc.sync.dma_start(out, store[:])

@@ -21,8 +21,9 @@ ROWS = 4
 TABLE_ROW = P - K // 32
 ALIGN = 256
 CUT = 512
+TAIL = 16
 FIRST = 256
-PIECES = [128,128,256,256,256]
+PIECES = [128,128,256,128,128,128,128]
 
 
 def tile_picked_idxput_add_p_kernel(tc, x_words, x_scales, mem, w1, offs, slot, out):
@@ -72,6 +73,7 @@ def tile_picked_idxput_add_p_kernel(tc, x_words, x_scales, mem, w1, offs, slot, 
         nc.vector.tensor_copy(late_code[:], word_table[:].bitcast(U32).indirect(offs_sb[:, CUT // LANES :]))
 
         y = pool.tile([P, S], F32, name="y", align_bytes=ALIGN)
+        y_tail = pool.tile([P, TAIL], F32, name="y_tail", align_bytes=ALIGN)
         lo = 0
         for width in PIECES:
             hi = lo + width
@@ -79,10 +81,16 @@ def tile_picked_idxput_add_p_kernel(tc, x_words, x_scales, mem, w1, offs, slot, 
             acc = psum.tile([P, width], F32, name=f"acc{lo}")
             nc.tensor.matmul_mx(out=acc[:], lhsT=w_code[:].bitcast(FP8X4), lhsT_scale=w_scale[:],
                                 rhs=code.bitcast(FP8X4), rhs_scale=x_scale[:, lo:hi], start=True, stop=True)
-            nc.scalar.copy(y[:, lo:hi], acc[:])
+            if hi < S:
+                nc.scalar.copy(y[:, lo:hi], acc[:])
+            else:
+                nc.scalar.copy(y[:, lo : S - TAIL], acc[:, : width - TAIL])
+                nc.scalar.copy(y_tail[:], acc[:, width - TAIL :])
             lo = hi
 
         for lo, hi in ((0, FIRST), (FIRST, S)):
+            if lo > 0:
+                nc.vector.tensor_copy(y[:, S - TAIL :], y_tail[:])
             nc.vector.tensor_tensor(store[:].indirect(slot_sb[:, lo // LANES : hi // LANES]), old[:, lo:hi], y[:, lo:hi],
                                     mybir.AluOpType.add)
         nc.sync.dma_start(out, store[:])

@@ -51,7 +51,10 @@ def tile_picked_idxput_add_p_kernel(tc, x_words, x_scales, mem, w1, offs, slot, 
         nc.sync.dma_start(w_raw[:], w1.rearrange("(p j) n -> p j n", j=PACK))
 
         w_grouped = pool.tile([P, N, PACK], BF16, name="w_grouped", align_bytes=ALIGN)
-        nc.scalar.copy(w_grouped[:].rearrange("p (c i) j -> p c j i", i=4), w_raw[:].rearrange("p j (c i) -> p c j i", i=4))
+        nc.scalar.copy(w_grouped[:, : N // 2, :].rearrange("p (c i) j -> p c j i", i=4),
+                       w_raw[:, :, : N // 2].rearrange("p j (c i) -> p c j i", i=4))
+        nc.gpsimd.tensor_scalar(w_grouped[:, N // 2 :, :], w_raw[:, :, N // 2 :].rearrange("p j n -> p n j"), 1.0, 0.0,
+                                mybir.AluOpType.mult, mybir.AluOpType.add)
 
         picked_scale = pool.tile([P, S], U8, name="picked_scale", align_bytes=ALIGN)
         nc.vector.tensor_copy(picked_scale[:], scale_table[:].indirect(offs_sb[:]))
@@ -68,7 +71,9 @@ def tile_picked_idxput_add_p_kernel(tc, x_words, x_scales, mem, w1, offs, slot, 
         nc.vector.tensor_copy(early_code[:], word_table[:].bitcast(U32).indirect(offs_sb[:, : CUT // LANES]))
         w_code = pool.tile([P, N], U32, name="w_code", align_bytes=ALIGN)
         w_scale = pool.tile([P, N], U8, name="w_scale", align_bytes=ALIGN)
-        nc.vector.quantize_mx(out=w_code[:].bitcast(FP8X4), scales=w_scale[:], in_=w_grouped[:].rearrange("p n j -> p (n j)"))
+        for cols in (slice(0, N // 2), slice(N // 2, N)):
+            nc.vector.quantize_mx(out=w_code[:, cols].bitcast(FP8X4), scales=w_scale[:, cols],
+                                  in_=w_grouped[:, cols, :].rearrange("p n j -> p (n j)"))
         late_code = pool.tile([P, S - CUT], U32, name="late_code", tag="staging", align_bytes=ALIGN)
         nc.vector.tensor_copy(late_code[:], word_table[:].bitcast(U32).indirect(offs_sb[:, CUT // LANES :]))
 

@@ -20,10 +20,10 @@ QUADRANTS, QUADRANT = 4, 32
 ROWS = 4
 TABLE_ROW = P - K // 32
 ALIGN = 256
-CUT = 512
+CUT = 448
 TAIL = 16
-FIRST = 256
-PIECES = [128,128,256,128,128,128,128]
+FIRST = 320
+PIECES = [128,128,64,128,128,256,128,64]
 
 
 def tile_picked_idxput_add_p_kernel(tc, x_words, x_scales, mem, w1, offs, slot, out):
@@ -58,7 +58,7 @@ def tile_picked_idxput_add_p_kernel(tc, x_words, x_scales, mem, w1, offs, slot, 
 
         picked_scale = pool.tile([P, S], U8, name="picked_scale", align_bytes=ALIGN)
         nc.vector.tensor_copy(picked_scale[:], scale_table[:].indirect(offs_sb[:]))
-        moves = [(q, cols) for cols in (slice(0, CUT), slice(CUT, S)) for q in range(QUADRANTS)]
+        moves = [(q, cols) for cols in (slice(0, S // 2), slice(S // 2, S)) for q in range(QUADRANTS)]
         for q, cols in moves:
             src_row, dst_row = TABLE_ROW + ROWS * q, QUADRANT * q
             nc.sync.dma_start(x_scale[dst_row : dst_row + ROWS, cols].bitcast(I32),

@@ -24,6 +24,7 @@ CUT = 448
 TAIL = 16
 FIRST = 320
 PIECES = [128,128,64,128,128,256,128,64]
+SHARE = N // 4
 
 
 def tile_picked_idxput_add_p_kernel(tc, x_words, x_scales, mem, w1, offs, slot, out):
@@ -51,10 +52,11 @@ def tile_picked_idxput_add_p_kernel(tc, x_words, x_scales, mem, w1, offs, slot, 
         nc.sync.dma_start(w_raw[:], w1.rearrange("(p j) n -> p j n", j=PACK))
 
         w_grouped = pool.tile([P, N, PACK], BF16, name="w_grouped", align_bytes=ALIGN)
-        nc.scalar.copy(w_grouped[:, : N // 2, :].rearrange("p (c i) j -> p c j i", i=4),
-                       w_raw[:, :, : N // 2].rearrange("p j (c i) -> p c j i", i=4))
-        nc.gpsimd.tensor_scalar(w_grouped[:, N // 2 :, :], w_raw[:, :, N // 2 :].rearrange("p j n -> p n j"), 1.0, 0.0,
+        nc.gpsimd.tensor_scalar(w_grouped[:, :SHARE, :], w_raw[:, :, :SHARE].rearrange("p j n -> p n j"), 1.0, 0.0,
                                 mybir.AluOpType.mult, mybir.AluOpType.add)
+        for cols in (slice(SHARE, N // 2), slice(N // 2, N)):
+            nc.scalar.copy(w_grouped[:, cols, :].rearrange("p (c i) j -> p c j i", i=4),
+                           w_raw[:, :, cols].rearrange("p j (c i) -> p c j i", i=4))
 
         picked_scale = pool.tile([P, S], U8, name="picked_scale", align_bytes=ALIGN)
         nc.vector.tensor_copy(picked_scale[:], scale_table[:].indirect(offs_sb[:]))

@@ -22,8 +22,9 @@ TABLE_ROW = P - K // 32
 ALIGN = 256
 CUT = 448
 TAIL = 16
-FIRST = 320
-PIECES = [128,128,64,128,128,256,128,64]
+LAST = 768
+FIRST = 256
+PIECES = [128,128,64,128,64,256,128,128]
 SHARE = N // 4
 
 
@@ -77,7 +78,9 @@ def tile_picked_idxput_add_p_kernel(tc, x_words, x_scales, mem, w1, offs, slot, 
             nc.vector.quantize_mx(out=w_code[:, cols].bitcast(FP8X4), scales=w_scale[:, cols],
                                   in_=w_grouped[:, cols, :].rearrange("p n j -> p (n j)"))
         late_code = pool.tile([P, S - CUT], U32, name="late_code", tag="staging", align_bytes=ALIGN)
-        nc.vector.tensor_copy(late_code[:], word_table[:].bitcast(U32).indirect(offs_sb[:, CUT // LANES :]))
+        for lo, hi in ((CUT, LAST), (LAST, S)):
+            nc.vector.tensor_copy(late_code[:, lo - CUT : hi - CUT],
+                                  word_table[:].bitcast(U32).indirect(offs_sb[:, lo // LANES : hi // LANES]))
 
         y = pool.tile([P, S], F32, name="y", align_bytes=ALIGN)
         y_tail = pool.tile([P, TAIL], F32, name="y_tail", align_bytes=ALIGN)

@@ -12,6 +12,7 @@ U32 = mybir.dt.uint32
 U16 = mybir.dt.uint16
 U8 = mybir.dt.uint8
 FP8X4 = mybir.dt.float8_e4m3fn_x4
+COPY = mybir.ActivationFunctionType.Copy
 
 P = 128
 PACK = 4
@@ -20,16 +21,20 @@ QUADRANTS, QUADRANT = 4, 32
 ROWS = 4
 TABLE_ROW = P - K // 32
 ALIGN = 256
-CUT = 448
-TAIL = 16
-LAST = 768
-FIRST = 256
-PIECES = [128,128,64,128,64,256,128,128]
-SHARE = N // 4
+SPANS = ((0, 256), (256, 640), (640, 1024))
+SPLIT = 640
+SHARE = 384
+STEP = 128
+CHUNKS = (512, 512, 384, 384, 256)
+ADD = mybir.AluOpType.add
 
 
 def tile_picked_idxput_add_p_kernel(tc, x_words, x_scales, mem, w1, offs, slot, out):
     nc = tc.nc
+
+    def part(offsets, lo, hi):
+        return offsets[:, lo // LANES : hi // LANES]
+
     with ExitStack() as ctx:
         pool = ctx.enter_context(tc.tile_pool(name="pool", bufs=1))
         psum = ctx.enter_context(tc.psum_pool(name="psum", bufs=1))
@@ -38,69 +43,85 @@ def tile_picked_idxput_add_p_kernel(tc, x_words, x_scales, mem, w1, offs, slot, 
         slot_sb = pool.tile([P, S // LANES], U16, name="slot_sb")
         scale_table = pool.tile([P, T], U8, name="scale_table", align_bytes=ALIGN)
         word_table = pool.tile([P, T], I32, name="word_table", align_bytes=ALIGN)
+        w_raw = pool.tile([P, PACK, N], F32, name="w_raw", tag="held", align_bytes=ALIGN)
         store = pool.tile([P, U], F32, name="store", align_bytes=ALIGN)
-        w_raw = pool.tile([P, PACK, N], F32, name="w_raw", tag="staging", align_bytes=ALIGN)
+        patch = pool.tile([P, U], F32, name="patch", align_bytes=ALIGN)
+        zeros = pool.tile([P, S - SPLIT], F32, name="zeros", align_bytes=ALIGN)
         x_scale = pool.tile([P, S], U8, name="x_scale", align_bytes=ALIGN)
 
         nc.vector.memset(scale_table[0:TABLE_ROW, :].bitcast(I32), 0)
         nc.vector.memset(x_scale[:].bitcast(I32), 0)
+        nc.gpsimd.memset(patch[:], 0.0)
 
         nc.sync.dma_start(offs_sb[:], offs)
         nc.scalar.dma_start(scale_table[TABLE_ROW:P, :].bitcast(I32), x_scales[0].bitcast(I32))
         nc.sync.dma_start(slot_sb[:], slot)
         nc.sync.dma_start(store[:], mem)
-        nc.sync.dma_start(word_table[:], x_words[0].rearrange("p n t -> p (n t)").bitcast(I32))
         nc.sync.dma_start(w_raw[:], w1.rearrange("(p j) n -> p j n", j=PACK))
+        nc.sync.dma_start(word_table[:], x_words[0].rearrange("p n t -> p (n t)").bitcast(I32))
 
-        w_grouped = pool.tile([P, N, PACK], BF16, name="w_grouped", align_bytes=ALIGN)
-        nc.gpsimd.tensor_scalar(w_grouped[:, :SHARE, :], w_raw[:, :, :SHARE].rearrange("p j n -> p n j"), 1.0, 0.0,
-                                mybir.AluOpType.mult, mybir.AluOpType.add)
-        for cols in (slice(SHARE, N // 2), slice(N // 2, N)):
-            nc.scalar.copy(w_grouped[:, cols, :].rearrange("p (c i) j -> p c j i", i=4),
-                           w_raw[:, :, cols].rearrange("p j (c i) -> p c j i", i=4))
-
+        nc.scalar.copy(zeros[:], patch[:, : S - SPLIT])
         picked_scale = pool.tile([P, S], U8, name="picked_scale", align_bytes=ALIGN)
         nc.vector.tensor_copy(picked_scale[:], scale_table[:].indirect(offs_sb[:]))
-        moves = [(q, cols) for cols in (slice(0, S // 2), slice(S // 2, S)) for q in range(QUADRANTS)]
-        for q, cols in moves:
+        moves = [(0, 0, S), (1, 0, S), (2, 0, S // 2), (3, 0, S), (2, S // 2, S)]
+        for q, lo, hi in moves:
             src_row, dst_row = TABLE_ROW + ROWS * q, QUADRANT * q
-            nc.sync.dma_start(x_scale[dst_row : dst_row + ROWS, cols].bitcast(I32),
-                              picked_scale[src_row : src_row + ROWS, cols].bitcast(I32))
+            nc.sync.dma_start(x_scale[dst_row : dst_row + ROWS, lo:hi].bitcast(I32),
+                              picked_scale[src_row : src_row + ROWS, lo:hi].bitcast(I32))
 
+        (a0, a1), (b0, b1), (c0, c1) = SPANS
+        old_a = pool.tile([P, a1], F32, name="old_a", align_bytes=ALIGN)
         old = pool.tile([P, S], F32, name="old", align_bytes=ALIGN)
-        nc.vector.tensor_copy(old[:], store[:].indirect(slot_sb[:]))
+        nc.scalar.activation(old[:, a1 : S - SHARE + a1], store[:].indirect(part(slot_sb, a1, S - SHARE + a1)), COPY)
+        nc.vector.tensor_copy(old_a[:], store[:].indirect(part(slot_sb, a0, a1)))
+        nc.vector.tensor_copy(old[:, S - SHARE + a1 :], store[:].indirect(part(slot_sb, S - SHARE + a1, S)))
+        nc.scalar.activation(store[:].indirect(part(slot_sb, SPLIT, S)), zeros[:], COPY)
 
-        early_code = pool.tile([P, CUT], U32, name="early_code", align_bytes=ALIGN)
-        nc.vector.tensor_copy(early_code[:], word_table[:].bitcast(U32).indirect(offs_sb[:, : CUT // LANES]))
+        w_grouped = pool.tile([P, N, PACK], BF16, name="w_grouped", tag="late", align_bytes=ALIGN)
+        nc.gpsimd.tensor_scalar(w_grouped[:], w_raw[:].rearrange("p j n -> p n j"), 1.0, 0.0, mybir.AluOpType.mult, ADD)
         w_code = pool.tile([P, N], U32, name="w_code", align_bytes=ALIGN)
         w_scale = pool.tile([P, N], U8, name="w_scale", align_bytes=ALIGN)
-        for cols in (slice(0, N // 2), slice(N // 2, N)):
-            nc.vector.quantize_mx(out=w_code[:, cols].bitcast(FP8X4), scales=w_scale[:, cols],
-                                  in_=w_grouped[:, cols, :].rearrange("p n j -> p (n j)"))
-        late_code = pool.tile([P, S - CUT], U32, name="late_code", tag="staging", align_bytes=ALIGN)
-        for lo, hi in ((CUT, LAST), (LAST, S)):
-            nc.vector.tensor_copy(late_code[:, lo - CUT : hi - CUT],
-                                  word_table[:].bitcast(U32).indirect(offs_sb[:, lo // LANES : hi // LANES]))
+        nc.vector.quantize_mx(out=w_code[:].bitcast(FP8X4), scales=w_scale[:],
+                              in_=w_grouped[:].rearrange("p n j -> p (n j)"))
 
-        y = pool.tile([P, S], F32, name="y", align_bytes=ALIGN)
-        y_tail = pool.tile([P, TAIL], F32, name="y_tail", align_bytes=ALIGN)
+        def project(acc, at, code, base, lo, hi):
+            nc.tensor.matmul_mx(out=acc[:, lo - at : hi - at], lhsT=w_code[:].bitcast(FP8X4), lhsT_scale=w_scale[:],
+                                rhs=code[:, lo - base : hi - base].bitcast(FP8X4),
+                                rhs_scale=x_scale[:, lo:hi], start=True, stop=True)
+
+        def pick_words(code, base, lo, hi):
+            nc.vector.tensor_copy(code[:, lo - base : hi - base], word_table[:].bitcast(U32).indirect(part(offs_sb, lo, hi)))
+
+        new = pool.tile([P, SPLIT], F32, name="new", align_bytes=ALIGN)
+        y = pool.tile([P, S - SPLIT], F32, name="y", align_bytes=ALIGN)
+        b_mid, late, c_mid = b0 + STEP, b0 + 2 * STEP, c1 - STEP
+        acc_a = psum.tile([P, a1 - a0], F32, name="acc_a")
+        acc_b = psum.tile([P, b1 - b0], F32, name="acc_b")
+        acc_c = psum.tile([P, c_mid - c0], F32, name="acc_c")
+        acc_d = psum.tile([P, c1 - c_mid], F32, name="acc_d")
+
+        code_a = pool.tile([P, b_mid], U32, name="code_a", tag="held", align_bytes=ALIGN)
+        code_b = pool.tile([P, STEP], U32, name="code_b", tag="late", align_bytes=ALIGN)
+        pick_words(code_a, a0, a0, a1)
+        pick_words(code_b, b_mid, b_mid, late)
+        pick_words(code_a, a0, b0, b_mid)
+        project(acc_a, a0, code_a, a0, a0, a1)
+        project(acc_b, b0, code_b, b_mid, b_mid, late)
+        project(acc_b, b0, code_a, a0, b0, b_mid)
+        nc.vector.tensor_tensor(new[:, a0:a1], acc_a[:], old_a[:], ADD)
+        nc.scalar.activation(store[:].indirect(part(slot_sb, a0, a1)), new[:, a0:a1], COPY)
+        code_c = pool.tile([P, S - late], U32, name="code_c", tag="late", align_bytes=ALIGN)
+        for acc, at, lo, hi in ((acc_b, b0, late, b1), (acc_c, c0, c0, c_mid), (acc_d, c_mid, c_mid, c1)):
+            pick_words(code_c, late, lo, hi)
+            project(acc, at, code_c, late, lo, hi)
+        nc.vector.tensor_tensor(new[:, b0:b1], acc_b[:], old[:, b0:b1], ADD)
+        nc.scalar.copy(y[:, : c_mid - c0], acc_c[:])
+        nc.vector.tensor_copy(y[:, c_mid - c0 :], acc_d[:])
+        nc.scalar.activation(store[:].indirect(part(slot_sb, b0, b1)), new[:, b0:b1], COPY)
+        nc.vector.tensor_tensor(patch[:].indirect(part(slot_sb, c0, c1)), old[:, c0:c1], y[:], ADD)
+
         lo = 0
-        for width in PIECES:
-            hi = lo + width
-            code = early_code[:, lo:hi] if hi <= CUT else late_code[:, lo - CUT : hi - CUT]
-            acc = psum.tile([P, width], F32, name=f"acc{lo}")
-            nc.tensor.matmul_mx(out=acc[:], lhsT=w_code[:].bitcast(FP8X4), lhsT_scale=w_scale[:],
-                                rhs=code.bitcast(FP8X4), rhs_scale=x_scale[:, lo:hi], start=True, stop=True)
-            if hi < S:
-                nc.scalar.copy(y[:, lo:hi], acc[:])
-            else:
-                nc.scalar.copy(y[:, lo : S - TAIL], acc[:, : width - TAIL])
-                nc.scalar.copy(y_tail[:], acc[:, width - TAIL :])
-            lo = hi
-
-        for lo, hi in ((0, FIRST), (FIRST, S)):
-            if lo > 0:
-                nc.vector.tensor_copy(y[:, S - TAIL :], y_tail[:])
-            nc.vector.tensor_tensor(store[:].indirect(slot_sb[:, lo // LANES : hi // LANES]), old[:, lo:hi], y[:, lo:hi],
-                                    mybir.AluOpType.add)
-        nc.sync.dma_start(out, store[:])
+        for width in CHUNKS:
+            nc.vector.tensor_tensor(patch[:, lo : lo + width], patch[:, lo : lo + width], store[:, lo : lo + width], ADD)
+            nc.sync.dma_start(out[:, lo : lo + width], patch[:, lo : lo + width])
+            lo = lo + width

@@ -23,8 +23,9 @@ TABLE_ROW = P - K // 32
 ALIGN = 256
 SPANS = ((0, 256), (256, 640), (640, 1024))
 SPLIT = 640
-SHARE = 384
+SHARE = 448
 STEP = 128
+FILL = 512
 CHUNKS = (512, 512, 384, 384, 256)
 ADD = mybir.AluOpType.add
 
@@ -46,12 +47,13 @@ def tile_picked_idxput_add_p_kernel(tc, x_words, x_scales, mem, w1, offs, slot, 
         w_raw = pool.tile([P, PACK, N], F32, name="w_raw", tag="held", align_bytes=ALIGN)
         store = pool.tile([P, U], F32, name="store", align_bytes=ALIGN)
         patch = pool.tile([P, U], F32, name="patch", align_bytes=ALIGN)
-        zeros = pool.tile([P, S - SPLIT], F32, name="zeros", align_bytes=ALIGN)
+        zeros = pool.tile([P, FILL], F32, name="zeros", tag="late", align_bytes=ALIGN)
         x_scale = pool.tile([P, S], U8, name="x_scale", align_bytes=ALIGN)
 
         nc.vector.memset(scale_table[0:TABLE_ROW, :].bitcast(I32), 0)
         nc.vector.memset(x_scale[:].bitcast(I32), 0)
-        nc.gpsimd.memset(patch[:], 0.0)
+        nc.vector.memset(zeros[:], 0.0)
+        nc.vector.memset(patch[:, :FILL], 0.0)
 
         nc.sync.dma_start(offs_sb[:], offs)
         nc.scalar.dma_start(scale_table[TABLE_ROW:P, :].bitcast(I32), x_scales[0].bitcast(I32))
@@ -60,7 +62,8 @@ def tile_picked_idxput_add_p_kernel(tc, x_words, x_scales, mem, w1, offs, slot, 
         nc.sync.dma_start(w_raw[:], w1.rearrange("(p j) n -> p j n", j=PACK))
         nc.sync.dma_start(word_table[:], x_words[0].rearrange("p n t -> p (n t)").bitcast(I32))
 
-        nc.scalar.copy(zeros[:], patch[:, : S - SPLIT])
+        for lo in range(FILL, U, FILL):
+            nc.scalar.copy(patch[:, lo : lo + FILL], zeros[:])
         picked_scale = pool.tile([P, S], U8, name="picked_scale", align_bytes=ALIGN)
         nc.vector.tensor_copy(picked_scale[:], scale_table[:].indirect(offs_sb[:]))
         moves = [(0, 0, S), (1, 0, S), (2, 0, S // 2), (3, 0, S), (2, S // 2, S)]
@@ -70,15 +73,13 @@ def tile_picked_idxput_add_p_kernel(tc, x_words, x_scales, mem, w1, offs, slot, 
                               picked_scale[src_row : src_row + ROWS, lo:hi].bitcast(I32))
 
         (a0, a1), (b0, b1), (c0, c1) = SPANS
-        old_a = pool.tile([P, a1], F32, name="old_a", align_bytes=ALIGN)
         old = pool.tile([P, S], F32, name="old", align_bytes=ALIGN)
-        nc.scalar.activation(old[:, a1 : S - SHARE + a1], store[:].indirect(part(slot_sb, a1, S - SHARE + a1)), COPY)
-        nc.vector.tensor_copy(old_a[:], store[:].indirect(part(slot_sb, a0, a1)))
-        nc.vector.tensor_copy(old[:, S - SHARE + a1 :], store[:].indirect(part(slot_sb, S - SHARE + a1, S)))
-        nc.scalar.activation(store[:].indirect(part(slot_sb, SPLIT, S)), zeros[:], COPY)
+        nc.vector.tensor_copy(old[:, :SHARE], store[:].indirect(part(slot_sb, 0, SHARE)))
+        nc.scalar.activation(old[:, SHARE:], store[:].indirect(part(slot_sb, SHARE, S)), COPY)
+        nc.scalar.activation(store[:].indirect(part(slot_sb, SPLIT, S)), patch[:, : S - SPLIT], COPY)
 
         w_grouped = pool.tile([P, N, PACK], BF16, name="w_grouped", tag="late", align_bytes=ALIGN)
-        nc.gpsimd.tensor_scalar(w_grouped[:], w_raw[:].rearrange("p j n -> p n j"), 1.0, 0.0, mybir.AluOpType.mult, ADD)
+        nc.vector.tensor_copy(w_grouped[:], w_raw[:].rearrange("p j n -> p n j"))
         w_code = pool.tile([P, N], U32, name="w_code", align_bytes=ALIGN)
         w_scale = pool.tile([P, N], U8, name="w_scale", align_bytes=ALIGN)
         nc.vector.quantize_mx(out=w_code[:].bitcast(FP8X4), scales=w_scale[:],
@@ -94,28 +95,27 @@ def tile_picked_idxput_add_p_kernel(tc, x_words, x_scales, mem, w1, offs, slot, 
 
         new = pool.tile([P, SPLIT], F32, name="new", align_bytes=ALIGN)
         y = pool.tile([P, S - SPLIT], F32, name="y", align_bytes=ALIGN)
-        b_mid, late, c_mid = b0 + STEP, b0 + 2 * STEP, c1 - STEP
+        b_mid, c_mid = b1 - STEP, c1 - STEP
         acc_a = psum.tile([P, a1 - a0], F32, name="acc_a")
         acc_b = psum.tile([P, b1 - b0], F32, name="acc_b")
         acc_c = psum.tile([P, c_mid - c0], F32, name="acc_c")
         acc_d = psum.tile([P, c1 - c_mid], F32, name="acc_d")
 
-        code_a = pool.tile([P, b_mid], U32, name="code_a", tag="held", align_bytes=ALIGN)
-        code_b = pool.tile([P, STEP], U32, name="code_b", tag="late", align_bytes=ALIGN)
+        code_a = pool.tile([P, a1 - a0], U32, name="code_a", tag="held", align_bytes=ALIGN)
+        code_b = pool.tile([P, b1 - b0], U32, name="code_b", tag="late", align_bytes=ALIGN)
         pick_words(code_a, a0, a0, a1)
-        pick_words(code_b, b_mid, b_mid, late)
-        pick_words(code_a, a0, b0, b_mid)
+        pick_words(code_b, b0, b0, b1)
         project(acc_a, a0, code_a, a0, a0, a1)
-        project(acc_b, b0, code_b, b_mid, b_mid, late)
-        project(acc_b, b0, code_a, a0, b0, b_mid)
-        nc.vector.tensor_tensor(new[:, a0:a1], acc_a[:], old_a[:], ADD)
+        project(acc_b, b0, code_b, b0, b0, b_mid)
+        project(acc_b, b0, code_b, b0, b_mid, b1)
+        nc.vector.tensor_tensor(new[:, a0:a1], acc_a[:], old[:, a0:a1], ADD)
         nc.scalar.activation(store[:].indirect(part(slot_sb, a0, a1)), new[:, a0:a1], COPY)
-        code_c = pool.tile([P, S - late], U32, name="code_c", tag="late", align_bytes=ALIGN)
-        for acc, at, lo, hi in ((acc_b, b0, late, b1), (acc_c, c0, c0, c_mid), (acc_d, c_mid, c_mid, c1)):
-            pick_words(code_c, late, lo, hi)
-            project(acc, at, code_c, late, lo, hi)
+        code_c = pool.tile([P, c1 - c0], U32, name="code_c", tag="held", align_bytes=ALIGN)
+        for acc, lo, hi in ((acc_c, c0, c_mid), (acc_d, c_mid, c1)):
+            pick_words(code_c, c0, lo, hi)
+            project(acc, lo, code_c, c0, lo, hi)
         nc.vector.tensor_tensor(new[:, b0:b1], acc_b[:], old[:, b0:b1], ADD)
-        nc.scalar.copy(y[:, : c_mid - c0], acc_c[:])
+        nc.vector.tensor_copy(y[:, : c_mid - c0], acc_c[:])
         nc.vector.tensor_copy(y[:, c_mid - c0 :], acc_d[:])
         nc.scalar.activation(store[:].indirect(part(slot_sb, b0, b1)), new[:, b0:b1], COPY)
         nc.vector.tensor_tensor(patch[:].indirect(part(slot_sb, c0, c1)), old[:, c0:c1], y[:], ADD)

@@ -23,7 +23,7 @@ TABLE_ROW = P - K // 32
 ALIGN = 256
 SPANS = ((0, 256), (256, 640), (640, 1024))
 SPLIT = 640
-SHARE = 448
+SHARE = 352
 STEP = 128
 FILL = 512
 CHUNKS = (512, 512, 384, 384, 256)
@@ -64,6 +64,8 @@ def tile_picked_idxput_add_p_kernel(tc, x_words, x_scales, mem, w1, offs, slot, 
 
         for lo in range(FILL, U, FILL):
             nc.scalar.copy(patch[:, lo : lo + FILL], zeros[:])
+        blank = pool.tile([P, S - SPLIT], F32, name="blank", align_bytes=ALIGN)
+        nc.scalar.copy(blank[:], zeros[:, : S - SPLIT])
         picked_scale = pool.tile([P, S], U8, name="picked_scale", align_bytes=ALIGN)
         nc.vector.tensor_copy(picked_scale[:], scale_table[:].indirect(offs_sb[:]))
         moves = [(0, 0, S), (1, 0, S), (2, 0, S // 2), (3, 0, S), (2, S // 2, S)]
@@ -76,7 +78,7 @@ def tile_picked_idxput_add_p_kernel(tc, x_words, x_scales, mem, w1, offs, slot, 
         old = pool.tile([P, S], F32, name="old", align_bytes=ALIGN)
         nc.vector.tensor_copy(old[:, :SHARE], store[:].indirect(part(slot_sb, 0, SHARE)))
         nc.scalar.activation(old[:, SHARE:], store[:].indirect(part(slot_sb, SHARE, S)), COPY)
-        nc.scalar.activation(store[:].indirect(part(slot_sb, SPLIT, S)), patch[:, : S - SPLIT], COPY)
+        nc.scalar.activation(store[:].indirect(part(slot_sb, SPLIT, S)), blank[:], COPY)
 
         w_grouped = pool.tile([P, N, PACK], BF16, name="w_grouped", tag="late", align_bytes=ALIGN)
         nc.vector.tensor_copy(w_grouped[:], w_raw[:].rearrange("p j n -> p n j"))

from contextlib import ExitStack

import concourse.mybir as mybir

K, T, S, N, U = 512, 2048, 1024, 128, 2048
FLOPS = 2 * K * N * S

F32 = mybir.dt.float32
BF16 = mybir.dt.bfloat16
I32 = mybir.dt.int32
U32 = mybir.dt.uint32
U16 = mybir.dt.uint16
U8 = mybir.dt.uint8
FP8X4 = mybir.dt.float8_e4m3fn_x4
COPY = mybir.ActivationFunctionType.Copy

P = 128
PACK = 4
LANES = 16
QUADRANTS, QUADRANT = 4, 32
ROWS = 4
TABLE_ROW = P - K // 32
ALIGN = 256
SPANS = ((0, 256), (256, 640), (640, 1024))
SPLIT = 640
SHARE = 352
STEP = 128
FILL = 512
CHUNKS = (512, 512, 384, 384, 256)
ADD = mybir.AluOpType.add


def tile_picked_idxput_add_p_kernel(tc, x_words, x_scales, mem, w1, offs, slot, out):
    nc = tc.nc

    def part(offsets, lo, hi):
        return offsets[:, lo // LANES : hi // LANES]

    with ExitStack() as ctx:
        pool = ctx.enter_context(tc.tile_pool(name="pool", bufs=1))
        psum = ctx.enter_context(tc.psum_pool(name="psum", bufs=1))

        offs_sb = pool.tile([P, S // LANES], U16, name="offs_sb")
        slot_sb = pool.tile([P, S // LANES], U16, name="slot_sb")
        scale_table = pool.tile([P, T], U8, name="scale_table", align_bytes=ALIGN)
        word_table = pool.tile([P, T], I32, name="word_table", align_bytes=ALIGN)
        w_raw = pool.tile([P, PACK, N], F32, name="w_raw", tag="held", align_bytes=ALIGN)
        store = pool.tile([P, U], F32, name="store", align_bytes=ALIGN)
        patch = pool.tile([P, U], F32, name="patch", align_bytes=ALIGN)
        zeros = pool.tile([P, FILL], F32, name="zeros", tag="late", align_bytes=ALIGN)
        x_scale = pool.tile([P, S], U8, name="x_scale", align_bytes=ALIGN)

        nc.vector.memset(scale_table[0:TABLE_ROW, :].bitcast(I32), 0)
        nc.vector.memset(x_scale[:].bitcast(I32), 0)
        nc.vector.memset(zeros[:], 0.0)
        nc.vector.memset(patch[:, :FILL], 0.0)

        nc.sync.dma_start(offs_sb[:], offs)
        nc.scalar.dma_start(scale_table[TABLE_ROW:P, :].bitcast(I32), x_scales[0].bitcast(I32))
        nc.sync.dma_start(slot_sb[:], slot)
        nc.sync.dma_start(store[:], mem)
        nc.sync.dma_start(w_raw[:], w1.rearrange("(p j) n -> p j n", j=PACK))
        nc.sync.dma_start(word_table[:], x_words[0].rearrange("p n t -> p (n t)").bitcast(I32))

        for lo in range(FILL, U, FILL):
            nc.scalar.copy(patch[:, lo : lo + FILL], zeros[:])
        blank = pool.tile([P, S - SPLIT], F32, name="blank", align_bytes=ALIGN)
        nc.scalar.copy(blank[:], zeros[:, : S - SPLIT])
        picked_scale = pool.tile([P, S], U8, name="picked_scale", align_bytes=ALIGN)
        nc.vector.tensor_copy(picked_scale[:], scale_table[:].indirect(offs_sb[:]))
        moves = [(0, 0, S), (1, 0, S), (2, 0, S // 2), (3, 0, S), (2, S // 2, S)]
        for q, lo, hi in moves:
            src_row, dst_row = TABLE_ROW + ROWS * q, QUADRANT * q
            nc.sync.dma_start(x_scale[dst_row : dst_row + ROWS, lo:hi].bitcast(I32),
                              picked_scale[src_row : src_row + ROWS, lo:hi].bitcast(I32))

        (a0, a1), (b0, b1), (c0, c1) = SPANS
        old = pool.tile([P, S], F32, name="old", align_bytes=ALIGN)
        nc.vector.tensor_copy(old[:, :SHARE], store[:].indirect(part(slot_sb, 0, SHARE)))
        nc.scalar.activation(old[:, SHARE:], store[:].indirect(part(slot_sb, SHARE, S)), COPY)
        nc.scalar.activation(store[:].indirect(part(slot_sb, SPLIT, S)), blank[:], COPY)

        w_grouped = pool.tile([P, N, PACK], BF16, name="w_grouped", tag="late", align_bytes=ALIGN)
        nc.vector.tensor_copy(w_grouped[:], w_raw[:].rearrange("p j n -> p n j"))
        w_code = pool.tile([P, N], U32, name="w_code", align_bytes=ALIGN)
        w_scale = pool.tile([P, N], U8, name="w_scale", align_bytes=ALIGN)
        nc.vector.quantize_mx(out=w_code[:].bitcast(FP8X4), scales=w_scale[:],
                              in_=w_grouped[:].rearrange("p n j -> p (n j)"))

        def project(acc, at, code, base, lo, hi):
            nc.tensor.matmul_mx(out=acc[:, lo - at : hi - at], lhsT=w_code[:].bitcast(FP8X4), lhsT_scale=w_scale[:],
                                rhs=code[:, lo - base : hi - base].bitcast(FP8X4),
                                rhs_scale=x_scale[:, lo:hi], start=True, stop=True)

        def pick_words(code, base, lo, hi):
            nc.vector.tensor_copy(code[:, lo - base : hi - base], word_table[:].bitcast(U32).indirect(part(offs_sb, lo, hi)))

        new = pool.tile([P, SPLIT], F32, name="new", align_bytes=ALIGN)
        y = pool.tile([P, S - SPLIT], F32, name="y", align_bytes=ALIGN)
        b_mid, c_mid = b1 - STEP, c1 - STEP
        acc_a = psum.tile([P, a1 - a0], F32, name="acc_a")
        acc_b = psum.tile([P, b1 - b0], F32, name="acc_b")
        acc_c = psum.tile([P, c_mid - c0], F32, name="acc_c")
        acc_d = psum.tile([P, c1 - c_mid], F32, name="acc_d")

        code_a = pool.tile([P, a1 - a0], U32, name="code_a", tag="held", align_bytes=ALIGN)
        code_b = pool.tile([P, b1 - b0], U32, name="code_b", tag="late", align_bytes=ALIGN)
        pick_words(code_a, a0, a0, a1)
        pick_words(code_b, b0, b0, b1)
        project(acc_a, a0, code_a, a0, a0, a1)
        project(acc_b, b0, code_b, b0, b0, b_mid)
        project(acc_b, b0, code_b, b0, b_mid, b1)
        nc.vector.tensor_tensor(new[:, a0:a1], acc_a[:], old[:, a0:a1], ADD)
        nc.scalar.activation(store[:].indirect(part(slot_sb, a0, a1)), new[:, a0:a1], COPY)
        code_c = pool.tile([P, c1 - c0], U32, name="code_c", tag="held", align_bytes=ALIGN)
        for acc, lo, hi in ((acc_c, c0, c_mid), (acc_d, c_mid, c1)):
            pick_words(code_c, c0, lo, hi)
            project(acc, lo, code_c, c0, lo, hi)
        nc.vector.tensor_tensor(new[:, b0:b1], acc_b[:], old[:, b0:b1], ADD)
        nc.vector.tensor_copy(y[:, : c_mid - c0], acc_c[:])
        nc.vector.tensor_copy(y[:, c_mid - c0 :], acc_d[:])
        nc.scalar.activation(store[:].indirect(part(slot_sb, b0, b1)), new[:, b0:b1], COPY)
        nc.vector.tensor_tensor(patch[:].indirect(part(slot_sb, c0, c1)), old[:, c0:c1], y[:], ADD)

        lo = 0
        for width in CHUNKS:
            nc.vector.tensor_tensor(patch[:, lo : lo + width], patch[:, lo : lo + width], store[:, lo : lo + width], ADD)
            nc.sync.dma_start(out[:, lo : lo + width], patch[:, lo : lo + width])
            lo = lo + width
